import numpy as np, ml_dtypes
CORES = [36,164,52,180,100,228,116,244]
N = 8
import mx_ref
BF = ml_dtypes.bfloat16
def entries(a):
    return np.ascontiguousarray(a.T).reshape(-1)
def table(e):
    return np.ascontiguousarray(np.reshape(e, (-1, 16)).T).astype(np.int32)
def cols(t, e):
    v = np.concatenate([t.reshape(128, -1, 4), np.zeros((128, 1, 4), BF)], axis=1)
    return np.ascontiguousarray(v[:, e]).reshape(128, -1)
def f(rng, *shape):
    return mx_ref.flush((rng.standard_normal(shape, dtype=np.float32) * np.exp2(rng.integers(-2, 3, shape[:-1] + (1,)))).astype(BF))
def wide(rng, *shape, cols=0):
    v = rng.standard_normal(shape, dtype=np.float32) * np.exp2(rng.integers(-12, 13, shape)).astype(np.float32)
    if cols: v *= np.repeat(np.exp2(rng.integers(-cols, cols + 1, shape[:-2] + (1, shape[-1] // 4))) * (rng.random(shape[:-2] + (1, shape[-1] // 4)) > 0.0625), 4, axis=-1).astype(np.float32)
    return mx_ref.flush(v.astype(BF))
T, B, NB, SUM = 512, 512, 2, 2176
SIDE = np.array([0 if c < 128 else 1 for c in CORES])
CAP = np.where(SIDE[:, None] == SIDE[None, :], 448, 96)
ST = np.cumsum(CAP, axis=1) - CAP
def lists(rng, alone=False, same=False, full=False, last=False):
    it, it2, ob, bag = np.full((N, SUM), -1), np.full((N, SUM), -1), np.full((N, SUM), -1), np.full((N, SUM), -1)
    one = rng.integers(0, T, N)
    none = rng.permutation(N) if alone else np.full(N, -1)
    for r in range(N):
        has = np.zeros((N, B), bool)
        free = np.where(np.arange(N) == none[r], 0, CAP[:, r])
        if full: has[:, rng.integers(0, B)] = True
        g = np.flatnonzero(~has.any(axis=0))
        has[rng.permutation(np.repeat(np.arange(N), free - has.sum(axis=1)))[:len(g)], g] = True
        for s in range(N):
            n = CAP[s, r]; h = has[s].sum()
            k = n if full else rng.integers(h, free[s] + 1)
            has[s, rng.permutation(np.flatnonzero(~has[s]))[:k - h]] = True
            j = np.flatnonzero(has[s]); c = rng.permutation(n)[:k]
            if last: j, c = j[::-1], np.sort(c)
            else: j = rng.permutation(j)
            u = np.full(k, one[s]) if same else rng.integers(0, T, k)
            v = (u + rng.integers(1, T, k)) % T if same else rng.integers(0, T, k)
            v = np.where(rng.random(k) < (1.0 if alone else 0.25), -1, v)
            it[s, ST[s, r] + c] = u; it2[s, ST[s, r] + c] = v; ob[s, ST[s, r] + c] = j; bag[r, ST[r, s] + c] = j
    return {"it": np.stack([table(e) for e in it]), "it2": np.stack([table(e) for e in it2]), "ob": np.stack([table(e) for e in ob]), "bag": np.stack([table(e) for e in bag])}
def setup_inputs(rng):
    return {"ex": f(rng, N, 128, 4 * T), "w": f(rng, N, 128, 512 * NB), **lists(rng)}
def setup_inputs_alone(rng):
    return {**setup_inputs(rng), **lists(rng, alone=True)}
def setup_inputs_full(rng):
    return {**setup_inputs(rng), **lists(rng, full=True)}
def setup_inputs_last(rng):
    return {**setup_inputs(rng), **lists(rng, last=True)}
def setup_inputs_same(rng):
    return {**setup_inputs(rng), **lists(rng, same=True)}
def setup_inputs_spread(rng):
    d = setup_inputs(rng); d["ex"] = wide(rng, N, 128, 4 * T, cols=6); return d
def check_inputs(d):
    b = []
    it, it2, ob, bag = [np.stack([entries(d[k][r]) for r in range(N)]) for k in ("it", "it2", "ob", "bag")]
    if it.min() < -1 or it.max() >= T: b.append("it")
    if it2.min() < -1 or it2.max() >= T: b.append("it2")
    if (it2[it < 0] != -1).any(): b.append("a second item in an empty slot")
    if ob.min() < -1 or ob.max() >= B: b.append("ob")
    if bag.min() < -1 or bag.max() >= B: b.append("bag")
    for r in range(N):
        for s in range(N):
            n = CAP[s, r]; u = it[s, ST[s, r]:ST[s, r] + n]; j = bag[r, ST[r, s]:ST[r, s] + n]
            if ((u < 0) != (j < 0)).any(): b.append("bag and it differ in their empty slots")
            if (ob[s, ST[s, r]:ST[s, r] + n] != j).any(): b.append("ob and bag differ")
            j = j[j >= 0]
            if len(set(j.tolist())) != len(j): b.append("a bag named twice")
        if not set(range(B)) <= set(bag[r].tolist()): b.append("a bag without parts")
    return b
def reference(ex, w, it, it2, ob, bag):
    y = np.zeros((N, 128, B * NB), np.float32)
    for r in range(N):
        W = [mx_ref.quantize(w[r][:, 512 * o:512 * o + 512]) for o in range(NB)]
        for s in range(N):
            n = CAP[s, r]
            u, v = entries(it[s])[ST[s, r]:ST[s, r] + n], entries(it2[s])[ST[s, r]:ST[s, r] + n]
            part = (cols(ex[s], u).astype(np.float32) + cols(ex[s], v).astype(np.float32)).astype(BF)
            P = mx_ref.quantize(part)
            j = entries(bag[r])[ST[r, s]:ST[r, s] + n]; used = j >= 0
            for o in range(NB): y[r][:, B * o + j[used]] += mx_ref.matmul(W[o], P)[:, used]
    return {"y": y}

@@ -1,0 +1,265 @@
+from concourse.bass import DstId, RemoteDMATransfer
+from concourse.mybir import AluOpType, ActivationFunctionType, dt
+
+A = AluOpType
+COPY = ActivationFunctionType.Copy
+NEAR, FAR, ITEMS, BAGS = 448, 96, 512, 512
+NC, FC = NEAR // 16, FAR // 16
+PITCH = 624
+
+SCRATCH = {
+    "e": ("sbuf", [128, 16 + 4 * ITEMS], "bfloat16"),
+    "wt": ("sbuf", [128, 1024], "bfloat16"),
+    "wq": ("sbuf", [128, 256], "float8_e4m3fn_x4"),
+    "wqs": ("sbuf", [128, 256], "uint8"),
+    "tbl": ("sbuf", [128, 520], "float32"),
+    "nk": ("sbuf", [128, NC], "int32"),
+    "nkb": ("sbuf", [128, 4, FC], "int32"),
+    "gi": ("sbuf", [128, NC], "int32"),
+    "gb": ("sbuf", [128, NC], "int32"),
+    "gio": ("sbuf", [128, NC], "uint16"),
+    "gx": ("sbuf", [128, NC], "int32"),
+    "gy": ("sbuf", [128, NC], "int32"),
+    "gr": ("sbuf", [128, NC], "int32"),
+    "gz": ("sbuf", [128, NC], "int32"),
+    "gbo": ("sbuf", [128, NC], "uint16"),
+    "lin": ("sbuf", [128, NEAR], "float32"),
+    "win": ("sbuf", [128, 1024], "float32"),
+    "hop": ("dram", [16, 192], "float32"),
+    "lst": ("sbuf", [128, 256], "float32"),
+    "lt1": ("sbuf", [128, 4, 34], "int32"),
+    "lt2": ("sbuf", [128, 4, 34], "int32"),
+    "ltb": ("sbuf", [128, 4, 34], "int32"),
+    "bz1": ("sbuf", [128, 4, FC], "int32"),
+    "bz2": ("sbuf", [128, 4, FC], "int32"),
+    "yof": ("sbuf", [128, 4, 2 * FC], "uint16"),
+    "yw": ("sbuf", [128, 2 * PITCH], "float32"),
+    "rf": ("sbuf", [128, 4, 192], "float32"),
+    "yt1": ("sbuf", [128, 192], "float32"),
+    "yt2": ("sbuf", [128, 192], "float32"),
+    "yt3": ("sbuf", [128, 192], "float32"),
+    "yo": ("sbuf", [128, 1024], "float32"),
+    "uf": ("sbuf", [128, 1536], "bfloat16"),
+    "pf": ("sbuf", [128, 1536], "bfloat16"),
+    "fc": ("sbuf", [128, 384], "float8_e4m3fn_x4"),
+    "fs": ("sbuf", [128, 384], "uint8"),
+    "lfc": ("sbuf", [128, 384], "float8_e4m3fn_x4"),
+    "lfs": ("sbuf", [128, 384], "uint8"),
+}
+for _t in range(4):
+    SCRATCH["cf%d" % _t] = ("sbuf", [128, 48], "uint16")
+    SCRATCH["of%d" % _t] = ("sbuf", [128, 256], "uint16")
+    SCRATCH["u%d" % _t] = ("sbuf", [128, 2048], "bfloat16")
+    SCRATCH["p%d" % _t] = ("sbuf", [128, 2048], "bfloat16")
+    SCRATCH["qc%d" % _t] = ("sbuf", [128, 512], "float8_e4m3fn_x4")
+    SCRATCH["qs%d" % _t] = ("sbuf", [128, 512], "uint8")
+    SCRATCH["ps%d" % _t] = ("psum", [128, 512], "float32")
+    if _t < 3:
+        SCRATCH["lc%d" % _t] = ("sbuf", [128, 512], "float8_e4m3fn_x4")
+        SCRATCH["ls%d" % _t] = ("sbuf", [128, 512], "uint8")
+
+SEMAPHORES = ["lg", "lu", "lex", "lw", "lb", "k", "kb", "mwin", "me", "my", "a1", "a2", "a3", "a4", "a5", "a6", "inv",
+              "b0", "ov", "oq", "wqd", "h0", "h1", "h2", "d0", "d1", "y0", "y1", "y2", "mo", "rc", "f0", "f1",
+              "g0", "g1", "st0", "st1", "off", "sent", "land0", "land1", "land2"]
+SEMAPHORES += ["ou%d" % t for t in range(4)] + ["s%d" % i for i in range(7)]
+for _a in range(4):
+    SEMAPHORES += ["u%d%d" % (_a, t) for t in range(4)] + ["pd%d" % _a, "q%d" % _a]
+
+
+def rank_program(g, core, T, topo):
+    rank = T.rank_of(core)
+    if rank is None:
+        return
+    S, V, SC, TE, SY = T.sem, g.vector, g.scalar, g.tensor, g.sync
+    cores = list(T.cores)
+    n = len(cores)
+    side = [topo.host(c) for c in cores]
+    mine = [r for r in range(n) if side[r] == side[rank]]
+    other = [r for r in range(n) if side[r] != side[rank]]
+    q = mine.index(rank)
+    cap = [NC if side[r] == side[rank] else FC for r in range(n)]
+    st = [sum(cap[:r]) for r in range(n)]
+    near = [mine[(q + 1 + a) % 4] for a in range(4)]
+    flo = st[other[0]]
+    assert [st[r] for r in other] == [flo + 34 * k for k in range(4)]
+
+    for k in range(8):
+        a, v = k // 2, k % 2
+        c = st[near[a]]
+        SY.dma_start(T.gi[16 * k:16 * k + 16, :], (T.it2 if v else T.it)[:, c:c + NC]).then_inc(S.lg, 16)
+        SC.dma_start(T.gb[16 * k:16 * k + 16, :], T.ob[:, c:c + NC]).then_inc(S.lg, 16)
+    for k in range(8):
+        SY.dma_start(T.lt1[16 * k:16 * k + 16, :, :], T.it[:, :]).then_inc(S.lu, 16)
+        SC.dma_start(T.lt2[16 * k:16 * k + 16, :, :], T.it2[:, :]).then_inc(S.lu, 16)
+    SY.wait_ge(S.me, 1)
+    SY.dma_start(T.e[:, 16:16 + 4 * ITEMS], T.ex[:, :]).then_inc(S.lex, 16)
+    SY.dma_start(T.wt[:, :], T.w[:, :]).then_inc(S.lw, 16)
+    for k in range(8):
+        SY.dma_start(T.ltb[16 * k:16 * k + 16, :, :], T.bag[:, :]).then_inc(S.lb, 16)
+
+    for b in range(4):
+        g.iota(T.nk[32 * b:32 * b + 32, :], [[-16, NC]], -512, -1).then_inc(S.k, 1)
+    g.wait_ge(S.k, 4)
+    g.iota(T.tbl[:, :], [[4, 520]], 12, 0, allow_small_or_imprecise_dtypes=True).then_inc(S.k, 1)
+    g.wait_ge(S.k, 5)
+    for b in range(4):
+        g.iota(T.nkb[32 * b:32 * b + 32, :, :], [[0, 4], [-16, FC]], -512, -1).then_inc(S.kb, 1)
+    V.memset(T.e[:, 0:16], 0.0).then_inc(S.me, 1)
+    V.memset(T.win[:, 0:512], 12.0).then_inc(S.mwin, 1)
+    V.memset(T.yw[:, :], 0.0).then_inc(S.my, 1)
+
+    V.wait_ge(S.lg, 256)
+    V.tensor_scalar(T.gio[:, :], T.gi[:, :], 1.0, None, A.add).then_inc(S.a1, 1)
+    V.tensor_scalar(T.gx[:, :], T.gb[:, :], 513.0, None, A.mult).then_inc(S.a2, 1)
+    V.wait_ge(S.k, 5)
+    V.tensor_tensor(T.gy[:, :], T.gb[:, :], T.nk[:, :], A.mult).then_inc(S.a2, 1)
+    V.wait_ge(S.a2, 2)
+    V.tensor_scalar(T.gr[:, :], T.gx[:, :], 4, 511, A.arith_shift_right, A.bitwise_and).then_inc(S.a3, 1)
+    V.wait_ge(S.a3, 1)
+    V.tensor_tensor(T.gz[:, :], T.gr[:, :], T.gy[:, :], A.max).then_inc(S.a4, 1)
+    V.wait_ge(S.a4, 1)
+    V.tensor_copy(T.gbo[:, :], T.gz[:, :]).then_inc(S.a5, 1)
+    V.wait_ge(S.lu, 256)
+    for t in range(4):
+        V.tensor_scalar(T["cf%d" % t][:, 0:24], T.lt1[:, :, flo:flo + FC], 4.0, 16.0 + t, A.mult, A.add).then_inc(S.b0, 1)
+        V.tensor_scalar(T["cf%d" % t][:, 24:48], T.lt2[:, :, flo:flo + FC], 4.0, 16.0 + t, A.mult, A.add).then_inc(S.b0, 1)
+    V.wait_ge(S.a5, 1)
+    V.wait_ge(S.a6, 1)
+    V.wait_ge(S.mwin, 1)
+    V.tensor_copy(T.win[:, 0:1024].indirect(T.gbo[:, 0:NC]), T.lin[:, :]).then_inc(S.inv, 1)
+
+    SC.wait_ge(S.a1, 1)
+    SC.wait_ge(S.k, 5)
+    SC.activation(T.lin[:, :], T.tbl[:, 0:520].indirect(T.gio[:, 0:NC]), COPY).then_inc(S.a6, 1)
+
+    SY.wait_ge(S.inv, 1)
+    for k in range(2):
+        for h in range(8):
+            SY.dma_start(T.lst[16 * h:16 * h + 16, 32 * k:32 * k + 32], T.win[16 * k:16 * k + 1, 0:512]).then_inc(S.h0, 16)
+    for k in range(2, 8):
+        SY.dma_start(T.hop[:, 32 * (k - 2):32 * (k - 1)], T.win[16 * k:16 * k + 1, 0:512]).then_inc(S.h1, 16)
+    SY.wait_ge(S.h1, 96)
+    for h in range(8):
+        SY.dma_start(T.lst[16 * h:16 * h + 16, 64:256], T.hop[:, :]).then_inc(S.h2, 16)
+
+    win_e = T.e[:, 0:16 + 4 * ITEMS]
+    SC.wait_ge(S.b0, 8)
+    SC.wait_ge(S.me, 1)
+    SC.wait_ge(S.lex, 16)
+    V.wait_ge(S.lex, 16)
+    V.wait_ge(S.me, 1)
+    V.wait_ge(S.b0, 8)
+    for t in range(4):
+        of = T["cf%d" % t]
+        SC.activation(T.uf[:, 384 * t:384 * t + 384], win_e.indirect(of[:, 0:24]), COPY).then_inc(S["ou%d" % t], 1)
+        V.wait_ge(S["ou%d" % t], 1)
+        V.tensor_tensor(T.pf[:, t:1536:4], win_e.indirect(of[:, 24:48]), T.uf[:, 384 * t:384 * t + 384], A.add).then_inc(S.ov, 1)
+    V.wait_ge(S.ov, 4)
+    V.quantize_mx(T.fc[:, :], T.fs[:, :], T.pf[:, :]).then_inc(S.oq, 1)
+
+    V.wait_ge(S.h0, 256)
+    for t in range(4):
+        V.tensor_scalar(T["of%d" % t][:, 0:64], T.lst[:, 0:64], float(t), None, A.add).then_inc(S.d0, 1)
+    SC.wait_ge(S.d0, 4)
+    V.wait_ge(S.lw, 16)
+    V.quantize_mx(T.wq[:, :], T.wqs[:, :], T.wt[:, :]).then_inc(S.wqd, 1)
+    V.wait_ge(S.lb, 128)
+    V.wait_ge(S.kb, 4)
+    V.tensor_tensor(T.bz1[:, :, :], T.ltb[:, :, flo:flo + FC], T.nkb[:, :, :], A.mult).then_inc(S.y0, 1)
+    V.wait_ge(S.y0, 1)
+    V.tensor_tensor(T.bz2[:, :, :], T.bz1[:, :, :], T.ltb[:, :, flo:flo + FC], A.max).then_inc(S.y1, 1)
+    V.wait_ge(S.y1, 1)
+    V.tensor_scalar(T.yof[:, :, 0:FC], T.bz2[:, :, :], 0.0, None, A.add).then_inc(S.y2, 1)
+    V.tensor_scalar(T.yof[:, :, FC:2 * FC], T.bz2[:, :, :], float(PITCH), None, A.add).then_inc(S.y2, 1)
+    V.wait_ge(S.d0, 4)
+
+    def tile(a):
+        u, p = T["u%d" % a], T["p%d" % a]
+        for t in range(4):
+            of = T["of%d" % t]
+            SC.activation(u[:, 512 * t:512 * t + 512], win_e.indirect(of[:, 64 * a:64 * a + 32]), COPY).then_inc(S["u%d%d" % (a, t)], 1)
+            V.wait_ge(S["u%d%d" % (a, t)], 1)
+            V.tensor_tensor(p[:, t:2048:4], win_e.indirect(of[:, 64 * a + 32:64 * a + 64]), u[:, 512 * t:512 * t + 512], A.add).then_inc(S["pd%d" % a], 1)
+            if a == 0 and t == 2:
+                V.wait_ge(S.h2, 128)
+                for i in range(4):
+                    V.tensor_scalar(T["of%d" % i][:, 64:256], T.lst[:, 64:256], float(i), None, A.add).then_inc(S.d1, 1)
+        V.wait_ge(S["pd%d" % a], 4)
+        V.quantize_mx(T["qc%d" % a][:, :], T["qs%d" % a][:, :], p[:, :]).then_inc(S["q%d" % a], 1)
+        if a == 0:
+            SC.wait_ge(S.d1, 4)
+            V.wait_ge(S.d1, 4)
+
+    for a in range(3):
+        tile(a)
+
+    SC.wait_ge(S.mo, 2)
+    for o in range(2):
+        SC.activation(T.rf[:, :, FAR * o:FAR * o + FAR], T["ps%d" % (2 + o)][:, 0:384], COPY).then_inc(S.rc, 1)
+    V.wait_ge(S.rc, 2)
+    V.wait_ge(S.y2, 2)
+    V.wait_ge(S.my, 1)
+    yw = T.yw[:, 0:2 * PITCH]
+    V.tensor_copy(yw.indirect(T.yof[:, 0, :]), T.rf[:, 0, :]).then_inc(S.s0, 1)
+    for k in range(1, 4):
+        V.wait_ge(S["s%d" % (2 * k - 2)], 1)
+        tmp = T["yt%d" % k]
+        V.tensor_tensor(tmp[:, :], yw.indirect(T.yof[:, k, :]), T.rf[:, k, :], A.add).then_inc(S["s%d" % (2 * k - 1)], 1)
+        V.wait_ge(S["s%d" % (2 * k - 1)], 1)
+        V.tensor_copy(yw.indirect(T.yof[:, k, :]), tmp[:, :]).then_inc(S["s%d" % (2 * k)], 1)
+    tile(3)
+
+    def mm(out, o, c, s, start, stop):
+        return TE.matmul_mx(out, T.wq[:, 128 * o:128 * o + 128], T.wqs[:, 128 * o:128 * o + 128], c, s, start, stop)
+
+    TE.wait_ge(S.wqd, 1)
+    TE.wait_ge(S.off, 16)
+    for o in range(2):
+        mm(T["ps%d" % (2 + o)][:, 0:384], o, T.lfc[:, :], T.lfs[:, :], True, True).then_inc(S.mo, 1)
+    for a in range(3):
+        TE.wait_ge(S["land%d" % a], 16)
+        for o in range(2):
+            mm(T["ps%d" % o][:, :], o, T["lc%d" % a][:, :], T["ls%d" % a][:, :], a == 0, False)
+    TE.wait_ge(S.q3, 1)
+    for o in range(2):
+        mm(T["ps%d" % o][:, :], o, T.qc3[:, :], T.qs3[:, :], False, True).then_inc(S["f%d" % o], 1)
+
+    V.wait_ge(S.s6, 1)
+    for o in range(2):
+        V.wait_ge(S["f%d" % o], 1)
+        V.tensor_tensor(T.yo[:, 512 * o:512 * o + 512], T["ps%d" % o][:, :], T.yw[:, PITCH * o:PITCH * o + 512], A.add).then_inc(S["g%d" % o], 1)
+        e = (SY, SC)[o]
+        e.wait_ge(S["g%d" % o], 1)
+        e.dma_start(T.y[:, 512 * o:512 * o + 512], T.yo[:, 512 * o:512 * o + 512]).then_inc(S["st%d" % o], 16)
+        e.wait_ge(S["st%d" % o], 16)
+
+    def mask(es):
+        m = 0
+        for x in es:
+            m |= 1 << x
+        return m
+
+    def far(src, dst, bits):
+        tr = []
+        for b, r in enumerate(other):
+            d = cores[r]
+            rid, pid = topo.addr(d, core)
+            es = topo.engines(core, d)
+            w = len(es) // 4
+            i, o = src[:, FAR * b:FAR * b + FAR], dst[:, FAR * q:FAR * q + FAR]
+            if bits:
+                i, o = i.bitcast(dt.uint8), o.bitcast(dt.uint8)
+            tr.append(RemoteDMATransfer(src=i, dst=o, dst_ids=[DstId(rid=rid, pnc=pid)], dma_engine_mask=mask(es[w * b:w * b + w]), remote_sem=S.off))
+        g.remote_dma_fused(tr, local_sem=S.sent)
+
+    g.wait_ge(S.oq, 1)
+    far(T.fc, T.lfc, True)
+    far(T.fs, T.lfs, False)
+    for a in range(3):
+        d = cores[near[a]]
+        rid, pid = topo.addr(d, core)
+        m = topo.mask(core, d)
+        g.wait_ge(S["q%d" % a], 1)
+        g.remote_dma(T["lc%d" % a][:, :].bitcast(dt.uint8), T["qc%d" % a][:, :].bitcast(dt.uint8), S["land%d" % a], S.sent, pid, rid, m)
+        g.remote_dma(T["ls%d" % a][:, :], T["qs%d" % a][:, :], S["land%d" % a], S.sent, pid, rid, m)
+    g.wait_ge(S.sent, 64)

@@ -13,6 +13,9 @@ SCRATCH = {
     "wq": ("sbuf", [128, 256], "float8_e4m3fn_x4"),
     "wqs": ("sbuf", [128, 256], "uint8"),
     "tbl": ("sbuf", [128, 520], "float32"),
+    "ti": ("sbuf", [128, 1], "int32"),
+    "tr": ("sbuf", [128, 1], "int32"),
+    "tp": ("sbuf", [128, 1], "float32"),
     "nk": ("sbuf", [128, NC], "int32"),
     "nkb": ("sbuf", [128, 4, FC], "int32"),
     "gi": ("sbuf", [128, NC], "int32"),
@@ -25,10 +28,7 @@ SCRATCH = {
     "gbo": ("sbuf", [128, NC], "uint16"),
     "lin": ("sbuf", [128, NEAR], "float32"),
     "win": ("sbuf", [128, 1024], "float32"),
-    "hop": ("dram", [16, 192], "float32"),
-    "lst": ("sbuf", [128, 256], "float32"),
-    "lt1": ("sbuf", [128, 4, 34], "int32"),
-    "lt2": ("sbuf", [128, 4, 34], "int32"),
+    "lf": ("sbuf", [128, 2, 4, 34], "int32"),
     "ltb": ("sbuf", [128, 4, 34], "int32"),
     "bz1": ("sbuf", [128, 4, FC], "int32"),
     "bz2": ("sbuf", [128, 4, FC], "int32"),
@@ -45,11 +45,15 @@ SCRATCH = {
     "fs": ("sbuf", [128, 384], "uint8"),
     "lfc": ("sbuf", [128, 384], "float8_e4m3fn_x4"),
     "lfs": ("sbuf", [128, 384], "uint8"),
+    "pf0": ("psum", [128, 512], "float32"),
+    "pf1": ("psum", [128, 512], "float32"),
 }
 for _t in range(4):
     SCRATCH["cf%d" % _t] = ("sbuf", [128, 48], "uint16")
+    SCRATCH["lst%d" % _t] = ("sbuf", [128, 256], "float32")
     SCRATCH["of%d" % _t] = ("sbuf", [128, 256], "uint16")
     SCRATCH["u%d" % _t] = ("sbuf", [128, 2048], "bfloat16")
+    SCRATCH["v%d" % _t] = ("sbuf", [128, 2048], "bfloat16")
     SCRATCH["p%d" % _t] = ("sbuf", [128, 2048], "bfloat16")
     SCRATCH["qc%d" % _t] = ("sbuf", [128, 512], "float8_e4m3fn_x4")
     SCRATCH["qs%d" % _t] = ("sbuf", [128, 512], "uint8")
@@ -58,12 +62,19 @@ for _t in range(4):
         SCRATCH["lc%d" % _t] = ("sbuf", [128, 512], "float8_e4m3fn_x4")
         SCRATCH["ls%d" % _t] = ("sbuf", [128, 512], "uint8")
 
-SEMAPHORES = ["lg", "lu", "lex", "lw", "lb", "k", "kb", "mwin", "me", "my", "a1", "a2", "a3", "a4", "a5", "a6", "inv",
-              "b0", "ov", "oq", "wqd", "h0", "h1", "h2", "d0", "d1", "y0", "y1", "y2", "mo", "rc", "f0", "f1",
-              "g0", "g1", "st0", "st1", "off", "sent", "land0", "land1", "land2"]
+SEMAPHORES = ["lg", "lu", "lex", "lw", "lb", "k", "kt", "kb", "mwin", "me", "my", "t1", "t2", "a1", "a2", "a3", "a4", "a5",
+              "a6", "inv", "b0", "ov", "oq", "wqd", "y0", "y1", "y2", "mo", "rc", "off", "sent"]
 SEMAPHORES += ["ou%d" % t for t in range(4)] + ["s%d" % i for i in range(7)]
 for _a in range(4):
-    SEMAPHORES += ["u%d%d" % (_a, t) for t in range(4)] + ["pd%d" % _a, "q%d" % _a]
+    SEMAPHORES += [x + str(_a) for x in ("hu", "hv", "cu", "cv", "pd", "f", "g", "st", "land")]
+    SEMAPHORES += [x + "%d%d" % (_a, i) for i in range(2) for x in ("q", "sa", "sb", "ad")]
+
+BOTH = [[], [(384, 512)], [(384, 512)], [(0, 128), (128, 256)]]
+VEC = [[(0, 256), (256, 512)], [(0, 192), (192, 384)], [(0, 256), (256, 384)], [(256, 384), (384, 512)]]
+QP = [[(0, 512, 2, [])], [(0, 512, 2, [0])], [(0, 256, 1, []), (256, 512, 2, [0])], [(0, 256, 0, [0, 1]), (256, 512, 2, [])]]
+S_ORDER = "v00 v01 b10 v10 v11 b20 v20 v21 b30 rf b31 v30 v31"
+V_ORDER = "a00 a01 c20 c21 q00 a10 a11 c30 c31 q10 a20 q20 a21 q21 s0 g1 s1 g2 s2 a30 g3 s3 q30 a31 y00 y10 q31 y01 y11"
+G_ORDER = "far +10 s00 +20 s10 +30 s20 s21 +31"
 
 
 def rank_program(g, core, T, topo):
@@ -89,8 +100,8 @@ def rank_program(g, core, T, topo):
         SY.dma_start(T.gi[16 * k:16 * k + 16, :], (T.it2 if v else T.it)[:, c:c + NC]).then_inc(S.lg, 16)
         SC.dma_start(T.gb[16 * k:16 * k + 16, :], T.ob[:, c:c + NC]).then_inc(S.lg, 16)
     for k in range(8):
-        SY.dma_start(T.lt1[16 * k:16 * k + 16, :, :], T.it[:, :]).then_inc(S.lu, 16)
-        SC.dma_start(T.lt2[16 * k:16 * k + 16, :, :], T.it2[:, :]).then_inc(S.lu, 16)
+        SY.dma_start(T.lf[16 * k:16 * k + 16, 0, :, :], T.it[:, :]).then_inc(S.lu, 16)
+        SC.dma_start(T.lf[16 * k:16 * k + 16, 1, :, :], T.it2[:, :]).then_inc(S.lu, 16)
     SY.wait_ge(S.me, 1)
     SY.dma_start(T.e[:, 16:16 + 4 * ITEMS], T.ex[:, :]).then_inc(S.lex, 16)
     SY.dma_start(T.wt[:, :], T.w[:, :]).then_inc(S.lw, 16)
@@ -102,6 +113,8 @@ def rank_program(g, core, T, topo):
     g.wait_ge(S.k, 4)
     g.iota(T.tbl[:, :], [[4, 520]], 12, 0, allow_small_or_imprecise_dtypes=True).then_inc(S.k, 1)
     g.wait_ge(S.k, 5)
+    g.iota(T.ti[:, :], [[0, 1]], 0, 1).then_inc(S.kt, 1)
+    g.wait_ge(S.kt, 1)
     for b in range(4):
         g.iota(T.nkb[32 * b:32 * b + 32, :, :], [[0, 4], [-16, FC]], -512, -1).then_inc(S.kb, 1)
     V.memset(T.e[:, 0:16], 0.0).then_inc(S.me, 1)
@@ -114,15 +127,18 @@ def rank_program(g, core, T, topo):
     V.wait_ge(S.k, 5)
     V.tensor_tensor(T.gy[:, :], T.gb[:, :], T.nk[:, :], A.mult).then_inc(S.a2, 1)
     V.wait_ge(S.a2, 2)
-    V.tensor_scalar(T.gr[:, :], T.gx[:, :], 4, 511, A.arith_shift_right, A.bitwise_and).then_inc(S.a3, 1)
+    V.tensor_scalar(T.gr[:, :], T.gx[:, :], 2, 511, A.arith_shift_right, A.bitwise_and).then_inc(S.a3, 1)
+    V.wait_ge(S.kt, 1)
+    V.tensor_scalar(T.tr[:, :], T.ti[:, :], 3, None, A.bitwise_and).then_inc(S.t1, 1)
     V.wait_ge(S.a3, 1)
     V.tensor_tensor(T.gz[:, :], T.gr[:, :], T.gy[:, :], A.max).then_inc(S.a4, 1)
+    V.wait_ge(S.t1, 1)
+    V.tensor_copy(T.tp[:, :], T.tr[:, :]).then_inc(S.t2, 1)
     V.wait_ge(S.a4, 1)
     V.tensor_copy(T.gbo[:, :], T.gz[:, :]).then_inc(S.a5, 1)
     V.wait_ge(S.lu, 256)
     for t in range(4):
-        V.tensor_scalar(T["cf%d" % t][:, 0:24], T.lt1[:, :, flo:flo + FC], 4.0, 16.0 + t, A.mult, A.add).then_inc(S.b0, 1)
-        V.tensor_scalar(T["cf%d" % t][:, 24:48], T.lt2[:, :, flo:flo + FC], 4.0, 16.0 + t, A.mult, A.add).then_inc(S.b0, 1)
+        V.tensor_scalar(T["cf%d" % t][:, :], T.lf[:, :, :, flo:flo + FC], 4.0, 16.0 + t, A.mult, A.add).then_inc(S.b0, 1)
     V.wait_ge(S.a5, 1)
     V.wait_ge(S.a6, 1)
     V.wait_ge(S.mwin, 1)
@@ -133,105 +149,148 @@ def rank_program(g, core, T, topo):
     SC.activation(T.lin[:, :], T.tbl[:, 0:520].indirect(T.gio[:, 0:NC]), COPY).then_inc(S.a6, 1)
 
     SY.wait_ge(S.inv, 1)
-    for k in range(2):
-        for h in range(8):
-            SY.dma_start(T.lst[16 * h:16 * h + 16, 32 * k:32 * k + 32], T.win[16 * k:16 * k + 1, 0:512]).then_inc(S.h0, 16)
-    for k in range(2, 8):
-        SY.dma_start(T.hop[:, 32 * (k - 2):32 * (k - 1)], T.win[16 * k:16 * k + 1, 0:512]).then_inc(S.h1, 16)
-    SY.wait_ge(S.h1, 96)
-    for h in range(8):
-        SY.dma_start(T.lst[16 * h:16 * h + 16, 64:256], T.hop[:, :]).then_inc(S.h2, 16)
+    for a in range(4):
+        for v in range(2):
+            k = 2 * a + v
+            for t in range(4):
+                SY.dma_start(T["lst%d" % a][t:128:4, 128 * v:128 * v + 128], T.win[16 * k:16 * k + 8, 0:512]).then_inc(S[("hu%d", "hv%d")[v] % a], 16)
+
+    def conv(a, v):
+        V.wait_ge(S[("hu%d", "hv%d")[v] % a], 64)
+        V.tensor_scalar(T["of%d" % a][:, 128 * v:128 * v + 128], T["lst%d" % a][:, 128 * v:128 * v + 128], T.tp[:, 0:1], None, A.add).then_inc(S[("cu%d", "cv%d")[v] % a], 1)
 
     win_e = T.e[:, 0:16 + 4 * ITEMS]
-    SC.wait_ge(S.b0, 8)
+    SC.wait_ge(S.b0, 4)
     SC.wait_ge(S.me, 1)
     SC.wait_ge(S.lex, 16)
-    V.wait_ge(S.lex, 16)
+    V.wait_ge(S.b0, 4)
     V.wait_ge(S.me, 1)
-    V.wait_ge(S.b0, 8)
-    for t in range(4):
-        of = T["cf%d" % t]
-        SC.activation(T.uf[:, 384 * t:384 * t + 384], win_e.indirect(of[:, 0:24]), COPY).then_inc(S["ou%d" % t], 1)
+    V.wait_ge(S.t2, 1)
+    V.wait_ge(S.lex, 16)
+
+    def far_first(e, t):
+        i, o = win_e.indirect(T["cf%d" % t][:, 0:24]), T.uf[:, 384 * t:384 * t + 384]
+        (V.tensor_copy(o, i) if e is V else SC.activation(o, i, COPY)).then_inc(S["ou%d" % t], 1)
+
+    for t in (0, 1, 2):
+        far_first(SC, t)
+    far_first(V, 3)
+    for t in (0, 3, 1, 2):
         V.wait_ge(S["ou%d" % t], 1)
-        V.tensor_tensor(T.pf[:, t:1536:4], win_e.indirect(of[:, 24:48]), T.uf[:, 384 * t:384 * t + 384], A.add).then_inc(S.ov, 1)
+        V.tensor_tensor(T.pf[:, t:1536:4], win_e.indirect(T["cf%d" % t][:, 24:48]), T.uf[:, 384 * t:384 * t + 384], A.add).then_inc(S.ov, 1)
+        if t == 1:
+            V.wait_ge(S.lb, 128)
+            V.wait_ge(S.kb, 4)
+            V.tensor_tensor(T.bz1[:, :, :], T.ltb[:, :, flo:flo + FC], T.nkb[:, :, :], A.mult).then_inc(S.y0, 1)
+            conv(0, 0)
+            V.wait_ge(S.y0, 1)
+            V.tensor_tensor(T.bz2[:, :, :], T.bz1[:, :, :], T.ltb[:, :, flo:flo + FC], A.max).then_inc(S.y1, 1)
+            conv(0, 1)
     V.wait_ge(S.ov, 4)
     V.quantize_mx(T.fc[:, :], T.fs[:, :], T.pf[:, :]).then_inc(S.oq, 1)
-
-    V.wait_ge(S.h0, 256)
-    for t in range(4):
-        V.tensor_scalar(T["of%d" % t][:, 0:64], T.lst[:, 0:64], float(t), None, A.add).then_inc(S.d0, 1)
-    SC.wait_ge(S.d0, 4)
+    conv(1, 0)
+    conv(1, 1)
     V.wait_ge(S.lw, 16)
     V.quantize_mx(T.wq[:, :], T.wqs[:, :], T.wt[:, :]).then_inc(S.wqd, 1)
-    V.wait_ge(S.lb, 128)
-    V.wait_ge(S.kb, 4)
-    V.tensor_tensor(T.bz1[:, :, :], T.ltb[:, :, flo:flo + FC], T.nkb[:, :, :], A.mult).then_inc(S.y0, 1)
-    V.wait_ge(S.y0, 1)
-    V.tensor_tensor(T.bz2[:, :, :], T.bz1[:, :, :], T.ltb[:, :, flo:flo + FC], A.max).then_inc(S.y1, 1)
     V.wait_ge(S.y1, 1)
     V.tensor_scalar(T.yof[:, :, 0:FC], T.bz2[:, :, :], 0.0, None, A.add).then_inc(S.y2, 1)
     V.tensor_scalar(T.yof[:, :, FC:2 * FC], T.bz2[:, :, :], float(PITCH), None, A.add).then_inc(S.y2, 1)
-    V.wait_ge(S.d0, 4)
 
-    def tile(a):
-        u, p = T["u%d" % a], T["p%d" % a]
-        for t in range(4):
-            of = T["of%d" % t]
-            SC.activation(u[:, 512 * t:512 * t + 512], win_e.indirect(of[:, 64 * a:64 * a + 32]), COPY).then_inc(S["u%d%d" % (a, t)], 1)
-            V.wait_ge(S["u%d%d" % (a, t)], 1)
-            V.tensor_tensor(p[:, t:2048:4], win_e.indirect(of[:, 64 * a + 32:64 * a + 64]), u[:, 512 * t:512 * t + 512], A.add).then_inc(S["pd%d" % a], 1)
-            if a == 0 and t == 2:
-                V.wait_ge(S.h2, 128)
-                for i in range(4):
-                    V.tensor_scalar(T["of%d" % i][:, 64:256], T.lst[:, 64:256], float(i), None, A.add).then_inc(S.d1, 1)
-        V.wait_ge(S["pd%d" % a], 4)
-        V.quantize_mx(T["qc%d" % a][:, :], T["qs%d" % a][:, :], p[:, :]).then_inc(S["q%d" % a], 1)
-        if a == 0:
-            SC.wait_ge(S.d1, 4)
-            V.wait_ge(S.d1, 4)
+    def items(a, v, lo, hi):
+        return win_e.indirect(T["of%d" % a][:, 128 * v + lo // 4:128 * v + hi // 4])
 
-    for a in range(3):
-        tile(a)
+    def first(a, i):
+        lo, hi = VEC[a][i]
+        SC.wait_ge(S["cu%d" % a], 1)
+        SC.activation(T["u%d" % a][:, 4 * lo:4 * hi], items(a, 0, lo, hi), COPY).then_inc(S["sa%d%d" % (a, i)], 1)
 
-    SC.wait_ge(S.mo, 2)
-    for o in range(2):
-        SC.activation(T.rf[:, :, FAR * o:FAR * o + FAR], T["ps%d" % (2 + o)][:, 0:384], COPY).then_inc(S.rc, 1)
-    V.wait_ge(S.rc, 2)
-    V.wait_ge(S.y2, 2)
-    V.wait_ge(S.my, 1)
+    def both(a, i):
+        lo, hi = BOTH[a][i]
+        SC.wait_ge(S["cu%d" % a], 1)
+        SC.activation(T["p%d" % a][:, 4 * lo:4 * hi], items(a, 0, lo, hi), COPY).then_inc(S["sb%d%d" % (a, i)], 1)
+        SC.wait_ge(S["cv%d" % a], 1)
+        SC.activation(T["v%d" % a][:, 4 * lo:4 * hi], items(a, 1, lo, hi), COPY).then_inc(S["sb%d%d" % (a, i)], 1)
+
+    for w in S_ORDER.split():
+        if w == "rf":
+            SC.wait_ge(S.mo, 2)
+            for o in range(2):
+                SC.activation(T.rf[:, :, FAR * o:FAR * o + FAR], T["pf%d" % o][:, 0:384], COPY).then_inc(S.rc, 1)
+        else:
+            (both if w[0] == "b" else first)(int(w[1]), int(w[2]))
+
+    def add(a, i):
+        lo, hi = VEC[a][i]
+        V.wait_ge(S["cv%d" % a], 1)
+        V.wait_ge(S["sa%d%d" % (a, i)], 1)
+        V.tensor_tensor(T["p%d" % a][:, 4 * lo:4 * hi], items(a, 1, lo, hi), T["u%d" % a][:, 4 * lo:4 * hi], A.add).then_inc(S["pd%d" % a], 1)
+
+    def quant(a, i):
+        lo, hi, need, dmas = QP[a][i]
+        if need:
+            V.wait_ge(S["pd%d" % a], need)
+        for j in dmas:
+            V.wait_ge(S["ad%d%d" % (a, j)], 16)
+        V.quantize_mx(T["qc%d" % a][:, lo:hi], T["qs%d" % a][:, lo:hi], T["p%d" % a][:, 4 * lo:4 * hi]).then_inc(S["q%d%d" % (a, i)], 1)
+
     yw = T.yw[:, 0:2 * PITCH]
-    V.tensor_copy(yw.indirect(T.yof[:, 0, :]), T.rf[:, 0, :]).then_inc(S.s0, 1)
-    for k in range(1, 4):
+
+    def scat(k):
+        if k == 0:
+            V.wait_ge(S.rc, 2)
+            V.wait_ge(S.y2, 2)
+            V.wait_ge(S.my, 1)
+        else:
+            V.wait_ge(S["s%d" % (2 * k - 1)], 1)
+        V.tensor_copy(yw.indirect(T.yof[:, k, :]), T["yt%d" % k][:, :] if k else T.rf[:, 0, :]).then_inc(S["s%d" % (2 * k)], 1)
+
+    def gath(k):
         V.wait_ge(S["s%d" % (2 * k - 2)], 1)
-        tmp = T["yt%d" % k]
-        V.tensor_tensor(tmp[:, :], yw.indirect(T.yof[:, k, :]), T.rf[:, k, :], A.add).then_inc(S["s%d" % (2 * k - 1)], 1)
-        V.wait_ge(S["s%d" % (2 * k - 1)], 1)
-        V.tensor_copy(yw.indirect(T.yof[:, k, :]), tmp[:, :]).then_inc(S["s%d" % (2 * k)], 1)
-    tile(3)
+        V.tensor_tensor(T["yt%d" % k][:, :], yw.indirect(T.yof[:, k, :]), T.rf[:, k, :], A.add).then_inc(S["s%d" % (2 * k - 1)], 1)
+
+    def ysum(o, h):
+        b, c = 2 * o + h, 512 * o + 256 * h
+        if b == 0:
+            V.wait_ge(S.s6, 1)
+        V.wait_ge(S["f%d" % b], 1)
+        V.tensor_tensor(T.yo[:, c:c + 256], T["ps%d" % b][:, 0:256], T.yw[:, PITCH * o + 256 * h:PITCH * o + 256 * h + 256], A.add).then_inc(S["g%d" % b], 1)
+
+    for w in V_ORDER.split():
+        if len(w) == 2:
+            (scat if w[0] == "s" else gath)(int(w[1]))
+        else:
+            {"a": add, "q": quant, "c": conv, "y": ysum}[w[0]](int(w[1]), int(w[2]))
 
     def mm(out, o, c, s, start, stop):
         return TE.matmul_mx(out, T.wq[:, 128 * o:128 * o + 128], T.wqs[:, 128 * o:128 * o + 128], c, s, start, stop)
 
+    def half(h, c, s, start, stop):
+        for o in range(2):
+            m = mm(T["ps%d" % (2 * o + h)][:, 0:256], o, c[:, 256 * h:256 * h + 256], s[:, 256 * h:256 * h + 256], start, stop)
+            if stop:
+                m.then_inc(S["f%d" % (2 * o + h)], 1)
+
     TE.wait_ge(S.wqd, 1)
     TE.wait_ge(S.off, 16)
     for o in range(2):
-        mm(T["ps%d" % (2 + o)][:, 0:384], o, T.lfc[:, :], T.lfs[:, :], True, True).then_inc(S.mo, 1)
-    for a in range(3):
+        mm(T["pf%d" % o][:, 0:384], o, T.lfc[:, :], T.lfs[:, :], True, True).then_inc(S.mo, 1)
+    for a in range(2):
         TE.wait_ge(S["land%d" % a], 16)
-        for o in range(2):
-            mm(T["ps%d" % o][:, :], o, T["lc%d" % a][:, :], T["ls%d" % a][:, :], a == 0, False)
-    TE.wait_ge(S.q3, 1)
-    for o in range(2):
-        mm(T["ps%d" % o][:, :], o, T.qc3[:, :], T.qs3[:, :], False, True).then_inc(S["f%d" % o], 1)
+        for h in range(2):
+            half(h, T["lc%d" % a], T["ls%d" % a], a == 0, False)
+    for h in range(2):
+        TE.wait_ge(S["land%d" % (2 + h)], 16)
+        half(h, T.lc2, T.ls2, False, False)
+        TE.wait_ge(S["q3%d" % h], 1)
+        half(h, T.qc3, T.qs3, False, True)
 
-    V.wait_ge(S.s6, 1)
-    for o in range(2):
-        V.wait_ge(S["f%d" % o], 1)
-        V.tensor_tensor(T.yo[:, 512 * o:512 * o + 512], T["ps%d" % o][:, :], T.yw[:, PITCH * o:PITCH * o + 512], A.add).then_inc(S["g%d" % o], 1)
-        e = (SY, SC)[o]
-        e.wait_ge(S["g%d" % o], 1)
-        e.dma_start(T.y[:, 512 * o:512 * o + 512], T.yo[:, 512 * o:512 * o + 512]).then_inc(S["st%d" % o], 16)
-        e.wait_ge(S["st%d" % o], 16)
+    for h in range(2):
+        for o in range(2):
+            b, c = 2 * o + h, 512 * o + 256 * h
+            SY.wait_ge(S["g%d" % b], 1)
+            SY.dma_start(T.y[:, c:c + 256], T.yo[:, c:c + 256]).then_inc(S["st%d" % b], 16)
+    for b in range(4):
+        SY.wait_ge(S["st%d" % b], 16)
 
     def mask(es):
         m = 0
@@ -252,14 +311,26 @@ def rank_program(g, core, T, topo):
             tr.append(RemoteDMATransfer(src=i, dst=o, dst_ids=[DstId(rid=rid, pnc=pid)], dma_engine_mask=mask(es[w * b:w * b + w]), remote_sem=S.off))
         g.remote_dma_fused(tr, local_sem=S.sent)
 
-    g.wait_ge(S.oq, 1)
-    far(T.fc, T.lfc, True)
-    far(T.fs, T.lfs, False)
-    for a in range(3):
+    def summed(a, i):
+        lo, hi = BOTH[a][i]
+        g.wait_ge(S["sb%d%d" % (a, i)], 2)
+        g.dma_start(T["p%d" % a][:, 4 * lo:4 * hi], T["v%d" % a][:, 4 * lo:4 * hi], accum_op=A.add).then_inc(S["ad%d%d" % (a, i)], 16)
+
+    def send(a, i):
+        lo, hi, _, _ = QP[a][i]
         d = cores[near[a]]
         rid, pid = topo.addr(d, core)
         m = topo.mask(core, d)
-        g.wait_ge(S["q%d" % a], 1)
-        g.remote_dma(T["lc%d" % a][:, :].bitcast(dt.uint8), T["qc%d" % a][:, :].bitcast(dt.uint8), S["land%d" % a], S.sent, pid, rid, m)
-        g.remote_dma(T["ls%d" % a][:, :], T["qs%d" % a][:, :], S["land%d" % a], S.sent, pid, rid, m)
-    g.wait_ge(S.sent, 64)
+        land = S["land%d" % (a + i)]
+        g.wait_ge(S["q%d%d" % (a, i)], 1)
+        g.remote_dma(T["lc%d" % a][:, lo:hi].bitcast(dt.uint8), T["qc%d" % a][:, lo:hi].bitcast(dt.uint8), land, S.sent, pid, rid, m)
+        g.remote_dma(T["ls%d" % a][:, lo:hi], T["qs%d" % a][:, lo:hi], land, S.sent, pid, rid, m)
+
+    for w in G_ORDER.split():
+        if w == "far":
+            g.wait_ge(S.oq, 1)
+            far(T.fc, T.lfc, True)
+            far(T.fs, T.lfs, False)
+        else:
+            (summed if w[0] == "+" else send)(int(w[1]), int(w[2]))
+    g.wait_ge(S.sent, 80)

from concourse.bass import DstId, RemoteDMATransfer
from concourse.mybir import AluOpType, ActivationFunctionType, dt

A = AluOpType
COPY = ActivationFunctionType.Copy
NEAR, FAR, ITEMS, BAGS = 448, 96, 512, 512
NC, FC = NEAR // 16, FAR // 16
PITCH = 624

SCRATCH = {
    "e": ("sbuf", [128, 16 + 4 * ITEMS], "bfloat16"),
    "wt": ("sbuf", [128, 1024], "bfloat16"),
    "wq": ("sbuf", [128, 256], "float8_e4m3fn_x4"),
    "wqs": ("sbuf", [128, 256], "uint8"),
    "tbl": ("sbuf", [128, 520], "float32"),
    "ti": ("sbuf", [128, 1], "int32"),
    "tr": ("sbuf", [128, 1], "int32"),
    "tp": ("sbuf", [128, 1], "float32"),
    "nk": ("sbuf", [128, NC], "int32"),
    "nkb": ("sbuf", [128, 4, FC], "int32"),
    "gi": ("sbuf", [128, NC], "int32"),
    "gb": ("sbuf", [128, NC], "int32"),
    "gio": ("sbuf", [128, NC], "uint16"),
    "gx": ("sbuf", [128, NC], "int32"),
    "gy": ("sbuf", [128, NC], "int32"),
    "gr": ("sbuf", [128, NC], "int32"),
    "gz": ("sbuf", [128, NC], "int32"),
    "gbo": ("sbuf", [128, NC], "uint16"),
    "lin": ("sbuf", [128, NEAR], "float32"),
    "win": ("sbuf", [128, 1024], "float32"),
    "lf": ("sbuf", [128, 2, 4, 34], "int32"),
    "ltb": ("sbuf", [128, 4, 34], "int32"),
    "bz1": ("sbuf", [128, 4, FC], "int32"),
    "bz2": ("sbuf", [128, 4, FC], "int32"),
    "yof": ("sbuf", [128, 4, 2 * FC], "uint16"),
    "yw": ("sbuf", [128, 2 * PITCH], "float32"),
    "rf": ("sbuf", [128, 4, 192], "float32"),
    "yt1": ("sbuf", [128, 192], "float32"),
    "yt2": ("sbuf", [128, 192], "float32"),
    "yt3": ("sbuf", [128, 192], "float32"),
    "yo": ("sbuf", [128, 1024], "float32"),
    "uf": ("sbuf", [128, 1536], "bfloat16"),
    "pf": ("sbuf", [128, 1536], "bfloat16"),
    "fc": ("sbuf", [128, 384], "float8_e4m3fn_x4"),
    "fs": ("sbuf", [128, 384], "uint8"),
    "lfc": ("sbuf", [128, 384], "float8_e4m3fn_x4"),
    "lfs": ("sbuf", [128, 384], "uint8"),
    "pf0": ("psum", [128, 512], "float32"),
    "pf1": ("psum", [128, 512], "float32"),
}
for _t in range(4):
    SCRATCH["cf%d" % _t] = ("sbuf", [128, 48], "uint16")
    SCRATCH["lst%d" % _t] = ("sbuf", [128, 256], "float32")
    SCRATCH["of%d" % _t] = ("sbuf", [128, 256], "uint16")
    SCRATCH["u%d" % _t] = ("sbuf", [128, 2048], "bfloat16")
    SCRATCH["v%d" % _t] = ("sbuf", [128, 2048], "bfloat16")
    SCRATCH["p%d" % _t] = ("sbuf", [128, 2048], "bfloat16")
    SCRATCH["qc%d" % _t] = ("sbuf", [128, 512], "float8_e4m3fn_x4")
    SCRATCH["qs%d" % _t] = ("sbuf", [128, 512], "uint8")
    SCRATCH["ps%d" % _t] = ("psum", [128, 512], "float32")
    if _t < 3:
        SCRATCH["lc%d" % _t] = ("sbuf", [128, 512], "float8_e4m3fn_x4")
        SCRATCH["ls%d" % _t] = ("sbuf", [128, 512], "uint8")

SEMAPHORES = ["lg", "lu", "lex", "lw", "lb", "k", "kt", "kb", "mwin", "me", "my", "t1", "t2", "a1", "a2", "a3", "a4", "a5",
              "a6", "inv", "b0", "ov", "oq", "wqd", "y0", "y1", "y2", "mo", "rc", "off", "sent"]
SEMAPHORES += ["ou%d" % t for t in range(4)] + ["s%d" % i for i in range(7)]
for _a in range(4):
    SEMAPHORES += [x + str(_a) for x in ("hu", "hv", "cu", "cv", "pd", "f", "g", "st", "land")]
    SEMAPHORES += [x + "%d%d" % (_a, i) for i in range(2) for x in ("q", "sa", "sb", "ad")]

BOTH = [[], [(384, 512)], [(384, 512)], [(0, 128), (128, 256)]]
VEC = [[(0, 256), (256, 512)], [(0, 192), (192, 384)], [(0, 256), (256, 384)], [(256, 384), (384, 512)]]
QP = [[(0, 512, 2, [])], [(0, 512, 2, [0])], [(0, 256, 1, []), (256, 512, 2, [0])], [(0, 256, 0, [0, 1]), (256, 512, 2, [])]]
S_ORDER = "v00 v01 b10 v10 v11 b20 v20 v21 b30 rf b31 v30 v31"
V_ORDER = "a00 a01 c20 c21 q00 a10 a11 c30 c31 q10 a20 q20 a21 q21 s0 g1 s1 g2 s2 a30 g3 s3 q30 a31 y00 y10 q31 y01 y11"
G_ORDER = "far +10 s00 +20 s10 +30 s20 s21 +31"


def rank_program(g, core, T, topo):
    rank = T.rank_of(core)
    if rank is None:
        return
    S, V, SC, TE, SY = T.sem, g.vector, g.scalar, g.tensor, g.sync
    cores = list(T.cores)
    n = len(cores)
    side = [topo.host(c) for c in cores]
    mine = [r for r in range(n) if side[r] == side[rank]]
    other = [r for r in range(n) if side[r] != side[rank]]
    q = mine.index(rank)
    cap = [NC if side[r] == side[rank] else FC for r in range(n)]
    st = [sum(cap[:r]) for r in range(n)]
    near = [mine[(q + 1 + a) % 4] for a in range(4)]
    flo = st[other[0]]
    assert [st[r] for r in other] == [flo + 34 * k for k in range(4)]

    for k in range(8):
        a, v = k // 2, k % 2
        c = st[near[a]]
        SY.dma_start(T.gi[16 * k:16 * k + 16, :], (T.it2 if v else T.it)[:, c:c + NC]).then_inc(S.lg, 16)
        SC.dma_start(T.gb[16 * k:16 * k + 16, :], T.ob[:, c:c + NC]).then_inc(S.lg, 16)
    for k in range(8):
        SY.dma_start(T.lf[16 * k:16 * k + 16, 0, :, :], T.it[:, :]).then_inc(S.lu, 16)
        SC.dma_start(T.lf[16 * k:16 * k + 16, 1, :, :], T.it2[:, :]).then_inc(S.lu, 16)
    SY.wait_ge(S.me, 1)
    SY.dma_start(T.e[:, 16:16 + 4 * ITEMS], T.ex[:, :]).then_inc(S.lex, 16)
    SY.dma_start(T.wt[:, :], T.w[:, :]).then_inc(S.lw, 16)
    for k in range(8):
        SY.dma_start(T.ltb[16 * k:16 * k + 16, :, :], T.bag[:, :]).then_inc(S.lb, 16)

    for b in range(4):
        g.iota(T.nk[32 * b:32 * b + 32, :], [[-16, NC]], -512, -1).then_inc(S.k, 1)
    g.wait_ge(S.k, 4)
    g.iota(T.tbl[:, :], [[4, 520]], 12, 0, allow_small_or_imprecise_dtypes=True).then_inc(S.k, 1)
    g.wait_ge(S.k, 5)
    g.iota(T.ti[:, :], [[0, 1]], 0, 1).then_inc(S.kt, 1)
    g.wait_ge(S.kt, 1)
    for b in range(4):
        g.iota(T.nkb[32 * b:32 * b + 32, :, :], [[0, 4], [-16, FC]], -512, -1).then_inc(S.kb, 1)
    V.memset(T.e[:, 0:16], 0.0).then_inc(S.me, 1)
    V.memset(T.win[:, 0:512], 12.0).then_inc(S.mwin, 1)
    V.memset(T.yw[:, :], 0.0).then_inc(S.my, 1)

    V.wait_ge(S.lg, 256)
    V.tensor_scalar(T.gio[:, :], T.gi[:, :], 1.0, None, A.add).then_inc(S.a1, 1)
    V.tensor_scalar(T.gx[:, :], T.gb[:, :], 513.0, None, A.mult).then_inc(S.a2, 1)
    V.wait_ge(S.k, 5)
    V.tensor_tensor(T.gy[:, :], T.gb[:, :], T.nk[:, :], A.mult).then_inc(S.a2, 1)
    V.wait_ge(S.a2, 2)
    V.tensor_scalar(T.gr[:, :], T.gx[:, :], 2, 511, A.arith_shift_right, A.bitwise_and).then_inc(S.a3, 1)
    V.wait_ge(S.kt, 1)
    V.tensor_scalar(T.tr[:, :], T.ti[:, :], 3, None, A.bitwise_and).then_inc(S.t1, 1)
    V.wait_ge(S.a3, 1)
    V.tensor_tensor(T.gz[:, :], T.gr[:, :], T.gy[:, :], A.max).then_inc(S.a4, 1)
    V.wait_ge(S.t1, 1)
    V.tensor_copy(T.tp[:, :], T.tr[:, :]).then_inc(S.t2, 1)
    V.wait_ge(S.a4, 1)
    V.tensor_copy(T.gbo[:, :], T.gz[:, :]).then_inc(S.a5, 1)
    V.wait_ge(S.lu, 256)
    for t in range(4):
        V.tensor_scalar(T["cf%d" % t][:, :], T.lf[:, :, :, flo:flo + FC], 4.0, 16.0 + t, A.mult, A.add).then_inc(S.b0, 1)
    V.wait_ge(S.a5, 1)
    V.wait_ge(S.a6, 1)
    V.wait_ge(S.mwin, 1)
    V.tensor_copy(T.win[:, 0:1024].indirect(T.gbo[:, 0:NC]), T.lin[:, :]).then_inc(S.inv, 1)

    SC.wait_ge(S.a1, 1)
    SC.wait_ge(S.k, 5)
    SC.activation(T.lin[:, :], T.tbl[:, 0:520].indirect(T.gio[:, 0:NC]), COPY).then_inc(S.a6, 1)

    SY.wait_ge(S.inv, 1)
    for a in range(4):
        for v in range(2):
            k = 2 * a + v
            for t in range(4):
                SY.dma_start(T["lst%d" % a][t:128:4, 128 * v:128 * v + 128], T.win[16 * k:16 * k + 8, 0:512]).then_inc(S[("hu%d", "hv%d")[v] % a], 16)

    def conv(a, v):
        V.wait_ge(S[("hu%d", "hv%d")[v] % a], 64)
        V.tensor_scalar(T["of%d" % a][:, 128 * v:128 * v + 128], T["lst%d" % a][:, 128 * v:128 * v + 128], T.tp[:, 0:1], None, A.add).then_inc(S[("cu%d", "cv%d")[v] % a], 1)

    win_e = T.e[:, 0:16 + 4 * ITEMS]
    SC.wait_ge(S.b0, 4)
    SC.wait_ge(S.me, 1)
    SC.wait_ge(S.lex, 16)
    V.wait_ge(S.b0, 4)
    V.wait_ge(S.me, 1)
    V.wait_ge(S.t2, 1)
    V.wait_ge(S.lex, 16)

    def far_first(e, t):
        i, o = win_e.indirect(T["cf%d" % t][:, 0:24]), T.uf[:, 384 * t:384 * t + 384]
        (V.tensor_copy(o, i) if e is V else SC.activation(o, i, COPY)).then_inc(S["ou%d" % t], 1)

    for t in (0, 1, 2):
        far_first(SC, t)
    far_first(V, 3)
    for t in (0, 3, 1, 2):
        V.wait_ge(S["ou%d" % t], 1)
        V.tensor_tensor(T.pf[:, t:1536:4], win_e.indirect(T["cf%d" % t][:, 24:48]), T.uf[:, 384 * t:384 * t + 384], A.add).then_inc(S.ov, 1)
        if t == 1:
            V.wait_ge(S.lb, 128)
            V.wait_ge(S.kb, 4)
            V.tensor_tensor(T.bz1[:, :, :], T.ltb[:, :, flo:flo + FC], T.nkb[:, :, :], A.mult).then_inc(S.y0, 1)
            conv(0, 0)
            V.wait_ge(S.y0, 1)
            V.tensor_tensor(T.bz2[:, :, :], T.bz1[:, :, :], T.ltb[:, :, flo:flo + FC], A.max).then_inc(S.y1, 1)
            conv(0, 1)
    V.wait_ge(S.ov, 4)
    V.quantize_mx(T.fc[:, :], T.fs[:, :], T.pf[:, :]).then_inc(S.oq, 1)
    conv(1, 0)
    conv(1, 1)
    V.wait_ge(S.lw, 16)
    V.quantize_mx(T.wq[:, :], T.wqs[:, :], T.wt[:, :]).then_inc(S.wqd, 1)
    V.wait_ge(S.y1, 1)
    V.tensor_scalar(T.yof[:, :, 0:FC], T.bz2[:, :, :], 0.0, None, A.add).then_inc(S.y2, 1)
    V.tensor_scalar(T.yof[:, :, FC:2 * FC], T.bz2[:, :, :], float(PITCH), None, A.add).then_inc(S.y2, 1)

    def items(a, v, lo, hi):
        return win_e.indirect(T["of%d" % a][:, 128 * v + lo // 4:128 * v + hi // 4])

    def first(a, i):
        lo, hi = VEC[a][i]
        SC.wait_ge(S["cu%d" % a], 1)
        SC.activation(T["u%d" % a][:, 4 * lo:4 * hi], items(a, 0, lo, hi), COPY).then_inc(S["sa%d%d" % (a, i)], 1)

    def both(a, i):
        lo, hi = BOTH[a][i]
        SC.wait_ge(S["cu%d" % a], 1)
        SC.activation(T["p%d" % a][:, 4 * lo:4 * hi], items(a, 0, lo, hi), COPY).then_inc(S["sb%d%d" % (a, i)], 1)
        SC.wait_ge(S["cv%d" % a], 1)
        SC.activation(T["v%d" % a][:, 4 * lo:4 * hi], items(a, 1, lo, hi), COPY).then_inc(S["sb%d%d" % (a, i)], 1)

    for w in S_ORDER.split():
        if w == "rf":
            SC.wait_ge(S.mo, 2)
            for o in range(2):
                SC.activation(T.rf[:, :, FAR * o:FAR * o + FAR], T["pf%d" % o][:, 0:384], COPY).then_inc(S.rc, 1)
        else:
            (both if w[0] == "b" else first)(int(w[1]), int(w[2]))

    def add(a, i):
        lo, hi = VEC[a][i]
        V.wait_ge(S["cv%d" % a], 1)
        V.wait_ge(S["sa%d%d" % (a, i)], 1)
        V.tensor_tensor(T["p%d" % a][:, 4 * lo:4 * hi], items(a, 1, lo, hi), T["u%d" % a][:, 4 * lo:4 * hi], A.add).then_inc(S["pd%d" % a], 1)

    def quant(a, i):
        lo, hi, need, dmas = QP[a][i]
        if need:
            V.wait_ge(S["pd%d" % a], need)
        for j in dmas:
            V.wait_ge(S["ad%d%d" % (a, j)], 16)
        V.quantize_mx(T["qc%d" % a][:, lo:hi], T["qs%d" % a][:, lo:hi], T["p%d" % a][:, 4 * lo:4 * hi]).then_inc(S["q%d%d" % (a, i)], 1)

    yw = T.yw[:, 0:2 * PITCH]

    def scat(k):
        if k == 0:
            V.wait_ge(S.rc, 2)
            V.wait_ge(S.y2, 2)
            V.wait_ge(S.my, 1)
        else:
            V.wait_ge(S["s%d" % (2 * k - 1)], 1)
        V.tensor_copy(yw.indirect(T.yof[:, k, :]), T["yt%d" % k][:, :] if k else T.rf[:, 0, :]).then_inc(S["s%d" % (2 * k)], 1)

    def gath(k):
        V.wait_ge(S["s%d" % (2 * k - 2)], 1)
        V.tensor_tensor(T["yt%d" % k][:, :], yw.indirect(T.yof[:, k, :]), T.rf[:, k, :], A.add).then_inc(S["s%d" % (2 * k - 1)], 1)

    def ysum(o, h):
        b, c = 2 * o + h, 512 * o + 256 * h
        if b == 0:
            V.wait_ge(S.s6, 1)
        V.wait_ge(S["f%d" % b], 1)
        V.tensor_tensor(T.yo[:, c:c + 256], T["ps%d" % b][:, 0:256], T.yw[:, PITCH * o + 256 * h:PITCH * o + 256 * h + 256], A.add).then_inc(S["g%d" % b], 1)

    for w in V_ORDER.split():
        if len(w) == 2:
            (scat if w[0] == "s" else gath)(int(w[1]))
        else:
            {"a": add, "q": quant, "c": conv, "y": ysum}[w[0]](int(w[1]), int(w[2]))

    def mm(out, o, c, s, start, stop):
        return TE.matmul_mx(out, T.wq[:, 128 * o:128 * o + 128], T.wqs[:, 128 * o:128 * o + 128], c, s, start, stop)

    def half(h, c, s, start, stop):
        for o in range(2):
            m = mm(T["ps%d" % (2 * o + h)][:, 0:256], o, c[:, 256 * h:256 * h + 256], s[:, 256 * h:256 * h + 256], start, stop)
            if stop:
                m.then_inc(S["f%d" % (2 * o + h)], 1)

    TE.wait_ge(S.wqd, 1)
    TE.wait_ge(S.off, 16)
    for o in range(2):
        mm(T["pf%d" % o][:, 0:384], o, T.lfc[:, :], T.lfs[:, :], True, True).then_inc(S.mo, 1)
    for a in range(2):
        TE.wait_ge(S["land%d" % a], 16)
        for h in range(2):
            half(h, T["lc%d" % a], T["ls%d" % a], a == 0, False)
    for h in range(2):
        TE.wait_ge(S["land%d" % (2 + h)], 16)
        half(h, T.lc2, T.ls2, False, False)
        TE.wait_ge(S["q3%d" % h], 1)
        half(h, T.qc3, T.qs3, False, True)

    for h in range(2):
        for o in range(2):
            b, c = 2 * o + h, 512 * o + 256 * h
            SY.wait_ge(S["g%d" % b], 1)
            SY.dma_start(T.y[:, c:c + 256], T.yo[:, c:c + 256]).then_inc(S["st%d" % b], 16)
    for b in range(4):
        SY.wait_ge(S["st%d" % b], 16)

    def mask(es):
        m = 0
        for x in es:
            m |= 1 << x
        return m

    def far(src, dst, bits):
        tr = []
        for b, r in enumerate(other):
            d = cores[r]
            rid, pid = topo.addr(d, core)
            es = topo.engines(core, d)
            w = len(es) // 4
            i, o = src[:, FAR * b:FAR * b + FAR], dst[:, FAR * q:FAR * q + FAR]
            if bits:
                i, o = i.bitcast(dt.uint8), o.bitcast(dt.uint8)
            tr.append(RemoteDMATransfer(src=i, dst=o, dst_ids=[DstId(rid=rid, pnc=pid)], dma_engine_mask=mask(es[w * b:w * b + w]), remote_sem=S.off))
        g.remote_dma_fused(tr, local_sem=S.sent)

    def summed(a, i):
        lo, hi = BOTH[a][i]
        g.wait_ge(S["sb%d%d" % (a, i)], 2)
        g.dma_start(T["p%d" % a][:, 4 * lo:4 * hi], T["v%d" % a][:, 4 * lo:4 * hi], accum_op=A.add).then_inc(S["ad%d%d" % (a, i)], 16)

    def send(a, i):
        lo, hi, _, _ = QP[a][i]
        d = cores[near[a]]
        rid, pid = topo.addr(d, core)
        m = topo.mask(core, d)
        land = S["land%d" % (a + i)]
        g.wait_ge(S["q%d%d" % (a, i)], 1)
        g.remote_dma(T["lc%d" % a][:, lo:hi].bitcast(dt.uint8), T["qc%d" % a][:, lo:hi].bitcast(dt.uint8), land, S.sent, pid, rid, m)
        g.remote_dma(T["ls%d" % a][:, lo:hi], T["qs%d" % a][:, lo:hi], land, S.sent, pid, rid, m)

    for w in G_ORDER.split():
        if w == "far":
            g.wait_ge(S.oq, 1)
            far(T.fc, T.lfc, True)
            far(T.fs, T.lfs, False)
        else:
            (summed if w[0] == "+" else send)(int(w[1]), int(w[2]))
    g.wait_ge(S.sent, 80)
